import numpy as np
import ml_dtypes


def mxq(x, axis, fmt="e4m3"):
    dtype, down = {"e4m3": (ml_dtypes.float8_e4m3fn, 7), "e5m2": (ml_dtypes.float8_e5m2, 14)}[fmt]
    v = np.moveaxis(np.asarray(x, np.float32).astype(ml_dtypes.bfloat16).astype(np.float64), axis, -1)
    blocks = v.reshape(v.shape[:-1] + (-1, 32))
    amax = np.abs(blocks).max(-1, keepdims=True)
    byte = np.maximum(np.where(amax > 0, np.frexp(amax)[1] - 1 + 127, 0) - down, 1)
    scale = np.exp2(byte - 127.0)
    codes = (blocks / scale).astype(np.float32).astype(dtype).astype(np.float64)
    return np.moveaxis((codes * scale).reshape(v.shape), -1, axis)


WIDE = False


def mx_kscale(k):
    if not WIDE:
        return np.ones(k)
    levels = np.array([10, -10, 5, -5, 0])
    if k % 512:
        return np.exp2(np.random.permutation(np.resize(levels, k // 32))).repeat(32)
    a = np.empty((k // 512, 16))
    for p in range(k // 512):
        a[p, :8] = np.random.permutation(np.resize(levels, 8))
        for g in range(8):
            far = levels[np.abs(levels - a[p, g]) >= 10]
            a[p, g + 8] = far[np.random.randint(len(far))]
    return np.exp2(a.ravel()).repeat(32)


def f64(x):
    return np.asarray(x).astype(np.float64)


def striped8(idx):
    return np.asarray(idx).reshape(8, -1, 16).transpose(0, 2, 1).reshape(128, -1).astype(np.uint16)


def unstriped8(offs):
    return offs.reshape(8, 16, -1).transpose(0, 2, 1).reshape(8, -1).astype(np.int64)


def pick8(x, idx, run):
    r = np.arange(len(x))
    return x[r[:, None], idx[r % (8 * run) // run]]


E2M1 = np.array([0.0, 0.5, 1.0, 1.5, 2.0, 3.0, 4.0, 6.0, -0.0, -0.5, -1.0, -1.5, -2.0, -3.0, -4.0, -6.0])


def pack_weight(w, fmt):
    k, n = w.shape
    w = f64(np.asarray(w, np.float32).astype(ml_dtypes.bfloat16)).reshape(k // 32, 32, n)
    amax = np.abs(w).max(1)
    if fmt == "e4m3":
        byte = np.frexp(amax)[1] - 1 + 127 - 7
    else:
        mant, ex = np.frexp(amax / 6.0)
        byte = np.where(mant > 0.5, ex, ex - 1) + 127
    byte = np.clip(np.where(amax > 0, byte, 1), 1, 254)
    scaled = (w * np.exp2(127.0 - byte)[:, None, :]).reshape(k, n).astype(np.float32)
    by_word = np.ascontiguousarray(scaled.reshape(k // 512, 128, 4, n).transpose(0, 1, 3, 2))
    if fmt == "e4m3":
        words = by_word.astype(ml_dtypes.float8_e4m3fn).view(np.uint8)
    else:
        c = by_word.astype(ml_dtypes.float4_e2m1fn).view(np.uint8) & 0xF
        words = (c[..., 0::2] | (c[..., 1::2] << 4)).reshape(k // 512, 128, 2 * n)
    return np.ascontiguousarray(words), np.ascontiguousarray(byte.astype(np.uint8).reshape(k // 512, 16, n))


def unpack_weight(words, scales, fmt):
    g, _, n = scales.shape
    words = np.ascontiguousarray(words).reshape(g, 128, n, -1)
    if fmt == "e4m3":
        vals = words.view(ml_dtypes.float8_e4m3fn).astype(np.float64)
    else:
        nib = np.empty((g, 128, n, 4), np.uint8)
        nib[..., 0::2] = words & 0xF
        nib[..., 1::2] = words >> 4
        vals = E2M1[nib]
    vals = vals * np.repeat(np.exp2(scales.astype(np.float64) - 127.0), 8, axis=1)[..., None]
    return vals.transpose(0, 1, 3, 2).reshape(g * 512, n)


D, T, I, Q = 512, 1024, 512, 128


def setup_inputs():
    n = np.random.standard_normal
    idx = np.stack([np.random.permutation(T)[:I] for _ in range(8)])
    idx2 = np.stack([np.random.permutation(T)[:I] for _ in range(8)])
    idx3 = np.stack([np.random.permutation(T)[:I] for _ in range(8)])
    idx4 = np.stack([np.random.permutation(T)[:I] for _ in range(8)])
    fd = mx_kscale(D)
    keysp = pack_weight(n((D, T)) / fd[:, None], "e4m3")
    return {
        "query": (n((D, Q)) * 1.0 / np.sqrt(D) * fd[:, None]).astype(np.float32),
        "keys_words": keysp[0],
        "keys_scales": keysp[1],
        "old": (1.0 * n((Q, T))).astype(np.float32),
        "offs": striped8(idx),
        "offs2": striped8(idx2),
        "offs3": striped8(idx3),
        "offs4": striped8(idx4),
    }


def reference(query, keys_words, keys_scales, old, offs, offs2, offs3, offs4):
    idx = unstriped8(offs)
    idx2 = unstriped8(offs2)
    idx3 = unstriped8(offs3)
    idx4 = unstriped8(offs4)
    keysu = unpack_weight(keys_words, keys_scales, "e4m3")
    queryq = mxq(f64(query), 0, "e4m3")
    a = queryq.T @ keysu
    w = pick8(a, idx, 16) * pick8(a, idx2, 16)
    f1 = np.zeros((Q, T))
    f1[np.arange(Q)[:, None], idx[np.arange(Q) % 128 // 16]] = w
    f2 = f1 + f64(old)
    y = np.maximum(pick8(f2, idx3, 16), pick8(f2, idx4, 16))
    return y

@@ -1,0 +1,138 @@
+from contextlib import ExitStack
+
+import concourse.mybir as mybir
+
+D, T, I, Q = 512, 1024, 512, 128
+FLOPS = 2 * D * T * Q
+
+F32 = mybir.dt.float32
+BF16 = mybir.dt.bfloat16
+I32 = mybir.dt.int32
+U32 = mybir.dt.uint32
+U16 = mybir.dt.uint16
+U8 = mybir.dt.uint8
+FP8X4 = mybir.dt.float8_e4m3fn_x4
+ALU = mybir.AluOpType
+COPY = mybir.ActivationFunctionType.Copy
+
+P = 128
+PACK = 4
+N_TILE = 256
+N_TILES = T // N_TILE
+WORD_SPANS = ((0, 256), (256, 512), (512, 1024))
+HALF = I // 2
+HALF_COLS = HALF // 16
+
+
+def tile_attend_pairproduct_lean_throughtwo_heads_kernel(
+    tc, query, keys_words, keys_scales, old, offs, offs2, offs3, offs4, out
+):
+    nc = tc.nc
+    with ExitStack() as ctx:
+        keep = ctx.enter_context(tc.tile_pool(name="keep", bufs=1))
+        psum = ctx.enter_context(tc.psum_pool(name="psum", bufs=1))
+
+        k_scales = keep.tile([P, N_TILE], U8, align_bytes=64)
+        nc.vector.memset(k_scales[:].bitcast(I32), 0)
+
+        q_raw = keep.tile([P, PACK, Q], F32)
+        nc.sync.dma_start(out=q_raw[:], in_=query.rearrange("(p j) q -> p j q", j=PACK))
+
+        scale_rows = keys_scales[0].bitcast(I32).rearrange("f (a c) -> a f c", a=N_TILES)
+        for quad in range(4):
+            nc.sync.dma_start(
+                out=k_scales[32 * quad : 32 * quad + 16, :].bitcast(I32),
+                in_=scale_rows[:, 4 * quad : 4 * quad + 4, :],
+            )
+
+        words = keys_words[0].rearrange("p n t -> p (n t)").bitcast(I32)
+        k_words = []
+        for u, (w0, w1) in enumerate(WORD_SPANS):
+            part = keep.tile([P, w1 - w0], I32, name=f"k_words{u}", tag=f"staging{u}", align_bytes=64)
+            nc.sync.dma_start(out=part[:], in_=words[:, w0:w1])
+            k_words.append(part)
+
+        lists = {}
+        for n, src in ((1, offs2), (0, offs), (2, offs3), (3, offs4)):
+            tile = keep.tile([P, I // 16], U16, name=f"list{n}")
+            nc.sync.dma_start(tile[:], src)
+            lists[n] = tile
+
+        def half(n, h):
+            return lists[n][:, h * HALF_COLS : (h + 1) * HALF_COLS]
+
+        f1 = keep.tile([P, T], F32)
+        nc.vector.memset(f1[:], 0.0)
+
+        q_codes = keep.tile([P, Q], U32, align_bytes=64)
+        q_scales = keep.tile([P, Q], U8, align_bytes=64)
+        q_bf = []
+        for h in range(2):
+            part = keep.tile([P, Q // 2, PACK], BF16, name=f"q_bf{h}", align_bytes=64)
+            dst = part[:].rearrange("p (c i) j -> p c j i", i=4)
+            src = q_raw[:, :, h * 64 : (h + 1) * 64].rearrange("p j (c i) -> p c j i", i=4)
+            if h == 0:
+                nc.vector.tensor_copy(out=dst, in_=src)
+            else:
+                nc.scalar.copy(dst, src)
+            q_bf.append(part)
+        for h in range(2):
+            nc.vector.quantize_mx(
+                out=q_codes[:, h * 64 : (h + 1) * 64].bitcast(FP8X4),
+                scales=q_scales[:, h * 64 : (h + 1) * 64],
+                in_=q_bf[h][:].rearrange("p q j -> p (q j)"),
+            )
+
+
+        a = keep.tile([P, T], F32)
+        start = 0
+        for n, n_cols in enumerate((256, 256, 256, 256)):
+            bank = psum.tile([P, n_cols], F32, name=f"bank{n}")
+            plane, s0 = divmod(start, N_TILE)
+            load = min(n, 2)
+            c0 = start - WORD_SPANS[load][0]
+            nc.tensor.matmul_mx(
+                out=bank[:],
+                lhsT=q_codes[:].bitcast(FP8X4),
+                lhsT_scale=q_scales[:],
+                rhs=k_words[load][:, c0 : c0 + n_cols].bitcast(FP8X4),
+                rhs_scale=k_scales[4 * plane : P, s0 : s0 + n_cols],
+                start=True,
+                stop=True,
+            )
+            cols = a[:, start : start + n_cols]
+            if n % 2 == 0:
+                nc.scalar.copy(cols, bank[:])
+            else:
+                nc.vector.tensor_copy(cols, bank[:])
+            start = start + n_cols
+
+        old_sb = keep.tile([P, T], F32, tag="staging0", align_bytes=64)
+        nc.sync.dma_start(out=old_sb[:], in_=old)
+
+        def vector_gather(name, window, offsets):
+            got = keep.tile([P, HALF], F32, name=name)
+            nc.vector.tensor_copy(got[:], window[:].indirect(offsets))
+            return got
+
+        def scalar_gather(name, window, offsets):
+            got = keep.tile([P, HALF], F32, name=name)
+            nc.scalar.activation(got[:], window[:].indirect(offsets), COPY)
+            return got
+
+        left0 = vector_gather("left0", a, half(0, 0))
+        right0 = scalar_gather("right0", a, half(1, 0))
+        left1 = scalar_gather("left1", a, half(0, 1))
+        right1 = scalar_gather("right1", a, half(1, 1))
+        nc.vector.tensor_tensor(f1[:].indirect(half(0, 0)), left0[:], right0[:], ALU.mult)
+        nc.vector.tensor_tensor(f1[:].indirect(half(0, 1)), left1[:], right1[:], ALU.mult)
+
+        f2 = keep.tile([P, T], F32)
+        nc.vector.tensor_tensor(f2[:], f1[:], old_sb[:], ALU.add)
+
+        third = [vector_gather(f"third{h}", f2, half(2, h)) for h in range(2)]
+        fourth = [scalar_gather(f"fourth{h}", f2, half(3, h)) for h in range(2)]
+        for h, queue in enumerate((nc.sync, nc.scalar)):
+            y = keep.tile([P, HALF], F32, name=f"y{h}")
+            nc.vector.tensor_tensor(y[:], third[h][:], fourth[h][:], ALU.max)
+            queue.dma_start(out=out[:, h * HALF : (h + 1) * HALF], in_=y[:])

@@ -1,6 +1,7 @@
 from contextlib import ExitStack
 
 import concourse.mybir as mybir
+from concourse.masks import make_identity
 
 D, T, I, Q = 512, 1024, 512, 128
 FLOPS = 2 * D * T * Q
@@ -17,11 +18,14 @@ COPY = mybir.ActivationFunctionType.Copy
 
 P = 128
 PACK = 4
-N_TILE = 256
-N_TILES = T // N_TILE
-WORD_SPANS = ((0, 256), (256, 512), (512, 1024))
+PLANE = 256
+PLANES = T // PLANE
+PASSES = (256, 256, 256, 128, 128)
+WORD_SPANS = ((0, 256), (256, 768), (768, 1024))
 HALF = I // 2
 HALF_COLS = HALF // 16
+STORES = ((0, 256), (256, 384), (384, 512))
+PSUM_SHARE = 688
 
 
 def tile_attend_pairproduct_lean_throughtwo_heads_kernel(
@@ -32,25 +36,31 @@ def tile_attend_pairproduct_lean_throughtwo_heads_kernel(
         keep = ctx.enter_context(tc.tile_pool(name="keep", bufs=1))
         psum = ctx.enter_context(tc.psum_pool(name="psum", bufs=1))
 
-        k_scales = keep.tile([P, N_TILE], U8, align_bytes=64)
+        k_scales = keep.tile([P, PLANE], U8, align_bytes=64)
         nc.vector.memset(k_scales[:].bitcast(I32), 0)
 
-        q_raw = keep.tile([P, PACK, Q], F32)
+        q_raw = keep.tile([P, PACK, Q], F32, tag="staging")
         nc.sync.dma_start(out=q_raw[:], in_=query.rearrange("(p j) q -> p j q", j=PACK))
 
-        scale_rows = keys_scales[0].bitcast(I32).rearrange("f (a c) -> a f c", a=N_TILES)
+        words = keys_words[0].rearrange("p n t -> p (n t)").bitcast(I32)
+        k_words = [
+            keep.tile([P, w1 - w0], I32, name=f"k_words{u}", align_bytes=64)
+            for u, (w0, w1) in enumerate(WORD_SPANS)
+        ]
+
+        def load_words(u):
+            w0, w1 = WORD_SPANS[u]
+            nc.sync.dma_start(out=k_words[u][:], in_=words[:, w0:w1])
+
+        load_words(0)
+        scale_rows = keys_scales[0].bitcast(I32).rearrange("f (a c) -> a f c", a=PLANES)
         for quad in range(4):
             nc.sync.dma_start(
                 out=k_scales[32 * quad : 32 * quad + 16, :].bitcast(I32),
                 in_=scale_rows[:, 4 * quad : 4 * quad + 4, :],
             )
-
-        words = keys_words[0].rearrange("p n t -> p (n t)").bitcast(I32)
-        k_words = []
-        for u, (w0, w1) in enumerate(WORD_SPANS):
-            part = keep.tile([P, w1 - w0], I32, name=f"k_words{u}", tag=f"staging{u}", align_bytes=64)
-            nc.sync.dma_start(out=part[:], in_=words[:, w0:w1])
-            k_words.append(part)
+        for u in range(1, len(WORD_SPANS)):
+            load_words(u)
 
         lists = {}
         for n, src in ((1, offs2), (0, offs), (2, offs3), (3, offs4)):
@@ -63,6 +73,8 @@ def tile_attend_pairproduct_lean_throughtwo_heads_kernel(
 
         f1 = keep.tile([P, T], F32)
         nc.vector.memset(f1[:], 0.0)
+        ident = keep.tile([P, P], F32)
+        make_identity(nc, ident[:])
 
         q_codes = keep.tile([P, Q], U32, align_bytes=64)
         q_scales = keep.tile([P, Q], U8, align_bytes=64)
@@ -83,13 +95,12 @@ def tile_attend_pairproduct_lean_throughtwo_heads_kernel(
                 in_=q_bf[h][:].rearrange("p q j -> p (q j)"),
             )
 
-
         a = keep.tile([P, T], F32)
         start = 0
-        for n, n_cols in enumerate((256, 256, 256, 256)):
+        for n, n_cols in enumerate(PASSES):
             bank = psum.tile([P, n_cols], F32, name=f"bank{n}")
-            plane, s0 = divmod(start, N_TILE)
-            load = min(n, 2)
+            plane, s0 = divmod(start, PLANE)
+            load = max(u for u, (w0, w1) in enumerate(WORD_SPANS) if w0 <= start)
             c0 = start - WORD_SPANS[load][0]
             nc.tensor.matmul_mx(
                 out=bank[:],
@@ -107,7 +118,7 @@ def tile_attend_pairproduct_lean_throughtwo_heads_kernel(
                 nc.vector.tensor_copy(cols, bank[:])
             start = start + n_cols
 
-        old_sb = keep.tile([P, T], F32, tag="staging0", align_bytes=64)
+        old_sb = keep.tile([P, T], F32, tag="staging")
         nc.sync.dma_start(out=old_sb[:], in_=old)
 
         def vector_gather(name, window, offsets):
@@ -122,17 +133,35 @@ def tile_attend_pairproduct_lean_throughtwo_heads_kernel(
 
         left0 = vector_gather("left0", a, half(0, 0))
         right0 = scalar_gather("right0", a, half(1, 0))
-        left1 = scalar_gather("left1", a, half(0, 1))
         right1 = scalar_gather("right1", a, half(1, 1))
+        left1 = scalar_gather("left1", a, half(0, 1))
         nc.vector.tensor_tensor(f1[:].indirect(half(0, 0)), left0[:], right0[:], ALU.mult)
         nc.vector.tensor_tensor(f1[:].indirect(half(0, 1)), left1[:], right1[:], ALU.mult)
 
         f2 = keep.tile([P, T], F32)
-        nc.vector.tensor_tensor(f2[:], f1[:], old_sb[:], ALU.add)
+        banks_old = []
+        for b, (c0, c1) in enumerate(((0, 512), (512, PSUM_SHARE))):
+            blocks = (c1 - c0 + P - 1) // P
+            turned = psum.tile([P, blocks, P], F32, name=f"turned{b}", tag=f"bank{b}")
+            for j in range(blocks):
+                nc.tensor.transpose(turned[:, j, :], old_sb[:, c0 + j * P : c0 + (j + 1) * P], ident[:])
+            old_t = keep.tile([P, blocks, P], F32, name=f"old_t{b}")
+            nc.scalar.copy(old_t[:], turned[:])
+            back = psum.tile([P, blocks * P], F32, name=f"back{b}", tag=f"bank{b + 2}")
+            for j in range(blocks):
+                nc.tensor.transpose(back[:, j * P : (j + 1) * P], old_t[:, j, :], ident[:])
+            banks_old.append((c0, c1, back))
+        nc.gpsimd.tensor_tensor(f2[:, PSUM_SHARE:], f1[:, PSUM_SHARE:], old_sb[:, PSUM_SHARE:], ALU.add)
+        for c0, c1, back in banks_old:
+            nc.vector.tensor_tensor(f2[:, c0:c1], f1[:, c0:c1], back[:, : c1 - c0], ALU.add)
+
 
         third = [vector_gather(f"third{h}", f2, half(2, h)) for h in range(2)]
         fourth = [scalar_gather(f"fourth{h}", f2, half(3, h)) for h in range(2)]
-        for h, queue in enumerate((nc.sync, nc.scalar)):
-            y = keep.tile([P, HALF], F32, name=f"y{h}")
-            nc.vector.tensor_tensor(y[:], third[h][:], fourth[h][:], ALU.max)
-            queue.dma_start(out=out[:, h * HALF : (h + 1) * HALF], in_=y[:])
+        for s, (c0, c1) in enumerate(STORES):
+            h, r0 = divmod(c0, HALF)
+            y = keep.tile([P, c1 - c0], F32, name=f"y{s}")
+            part = slice(r0, r0 + c1 - c0)
+            nc.vector.tensor_tensor(y[:], third[h][:, part], fourth[h][:, part], ALU.max)
+            queue = nc.sync if s % 2 == 0 else nc.scalar
+            queue.dma_start(out=out[:, c0:c1], in_=y[:])

@@ -24,8 +24,8 @@ PASSES = (256, 256, 256, 128, 128)
 WORD_SPANS = ((0, 256), (256, 768), (768, 1024))
 HALF = I // 2
 HALF_COLS = HALF // 16
-STORES = ((0, 256), (256, 384), (384, 512))
-PSUM_SHARE = 688
+STORES = ((0, 256), (256, 512))
+PSUM_SHARE = 768
 
 
 def tile_attend_pairproduct_lean_throughtwo_heads_kernel(
@@ -71,10 +71,11 @@ def tile_attend_pairproduct_lean_throughtwo_heads_kernel(
         def half(n, h):
             return lists[n][:, h * HALF_COLS : (h + 1) * HALF_COLS]
 
+        ident = keep.tile([P, P], F32)
+        nc.vector.memset(ident[:], 0.0)
+        make_identity(nc, ident[:], nomemset=True)
         f1 = keep.tile([P, T], F32)
         nc.vector.memset(f1[:], 0.0)
-        ident = keep.tile([P, P], F32)
-        make_identity(nc, ident[:])
 
         q_codes = keep.tile([P, Q], U32, align_bytes=64)
         q_scales = keep.tile([P, Q], U8, align_bytes=64)

from contextlib import ExitStack

import concourse.mybir as mybir
from concourse.masks import make_identity

D, T, I, Q = 512, 1024, 512, 128
FLOPS = 2 * D * T * Q

F32 = mybir.dt.float32
BF16 = mybir.dt.bfloat16
I32 = mybir.dt.int32
U32 = mybir.dt.uint32
U16 = mybir.dt.uint16
U8 = mybir.dt.uint8
FP8X4 = mybir.dt.float8_e4m3fn_x4
ALU = mybir.AluOpType
COPY = mybir.ActivationFunctionType.Copy

P = 128
PACK = 4
PLANE = 256
PLANES = T // PLANE
PASSES = (256, 256, 256, 128, 128)
WORD_SPANS = ((0, 256), (256, 768), (768, 1024))
HALF = I // 2
HALF_COLS = HALF // 16
STORES = ((0, 256), (256, 512))
PSUM_SHARE = 768


def tile_attend_pairproduct_lean_throughtwo_heads_kernel(
    tc, query, keys_words, keys_scales, old, offs, offs2, offs3, offs4, out
):
    nc = tc.nc
    with ExitStack() as ctx:
        keep = ctx.enter_context(tc.tile_pool(name="keep", bufs=1))
        psum = ctx.enter_context(tc.psum_pool(name="psum", bufs=1))

        k_scales = keep.tile([P, PLANE], U8, align_bytes=64)
        nc.vector.memset(k_scales[:].bitcast(I32), 0)

        q_raw = keep.tile([P, PACK, Q], F32, tag="staging")
        nc.sync.dma_start(out=q_raw[:], in_=query.rearrange("(p j) q -> p j q", j=PACK))

        words = keys_words[0].rearrange("p n t -> p (n t)").bitcast(I32)
        k_words = [
            keep.tile([P, w1 - w0], I32, name=f"k_words{u}", align_bytes=64)
            for u, (w0, w1) in enumerate(WORD_SPANS)
        ]

        def load_words(u):
            w0, w1 = WORD_SPANS[u]
            nc.sync.dma_start(out=k_words[u][:], in_=words[:, w0:w1])

        load_words(0)
        scale_rows = keys_scales[0].bitcast(I32).rearrange("f (a c) -> a f c", a=PLANES)
        for quad in range(4):
            nc.sync.dma_start(
                out=k_scales[32 * quad : 32 * quad + 16, :].bitcast(I32),
                in_=scale_rows[:, 4 * quad : 4 * quad + 4, :],
            )
        for u in range(1, len(WORD_SPANS)):
            load_words(u)

        lists = {}
        for n, src in ((1, offs2), (0, offs), (2, offs3), (3, offs4)):
            tile = keep.tile([P, I // 16], U16, name=f"list{n}")
            nc.sync.dma_start(tile[:], src)
            lists[n] = tile

        def half(n, h):
            return lists[n][:, h * HALF_COLS : (h + 1) * HALF_COLS]

        ident = keep.tile([P, P], F32)
        nc.vector.memset(ident[:], 0.0)
        make_identity(nc, ident[:], nomemset=True)
        f1 = keep.tile([P, T], F32)
        nc.vector.memset(f1[:], 0.0)

        q_codes = keep.tile([P, Q], U32, align_bytes=64)
        q_scales = keep.tile([P, Q], U8, align_bytes=64)
        q_bf = []
        for h in range(2):
            part = keep.tile([P, Q // 2, PACK], BF16, name=f"q_bf{h}", align_bytes=64)
            dst = part[:].rearrange("p (c i) j -> p c j i", i=4)
            src = q_raw[:, :, h * 64 : (h + 1) * 64].rearrange("p j (c i) -> p c j i", i=4)
            if h == 0:
                nc.vector.tensor_copy(out=dst, in_=src)
            else:
                nc.scalar.copy(dst, src)
            q_bf.append(part)
        for h in range(2):
            nc.vector.quantize_mx(
                out=q_codes[:, h * 64 : (h + 1) * 64].bitcast(FP8X4),
                scales=q_scales[:, h * 64 : (h + 1) * 64],
                in_=q_bf[h][:].rearrange("p q j -> p (q j)"),
            )

        a = keep.tile([P, T], F32)
        start = 0
        for n, n_cols in enumerate(PASSES):
            bank = psum.tile([P, n_cols], F32, name=f"bank{n}")
            plane, s0 = divmod(start, PLANE)
            load = max(u for u, (w0, w1) in enumerate(WORD_SPANS) if w0 <= start)
            c0 = start - WORD_SPANS[load][0]
            nc.tensor.matmul_mx(
                out=bank[:],
                lhsT=q_codes[:].bitcast(FP8X4),
                lhsT_scale=q_scales[:],
                rhs=k_words[load][:, c0 : c0 + n_cols].bitcast(FP8X4),
                rhs_scale=k_scales[4 * plane : P, s0 : s0 + n_cols],
                start=True,
                stop=True,
            )
            cols = a[:, start : start + n_cols]
            if n % 2 == 0:
                nc.scalar.copy(cols, bank[:])
            else:
                nc.vector.tensor_copy(cols, bank[:])
            start = start + n_cols

        old_sb = keep.tile([P, T], F32, tag="staging")
        nc.sync.dma_start(out=old_sb[:], in_=old)

        def vector_gather(name, window, offsets):
            got = keep.tile([P, HALF], F32, name=name)
            nc.vector.tensor_copy(got[:], window[:].indirect(offsets))
            return got

        def scalar_gather(name, window, offsets):
            got = keep.tile([P, HALF], F32, name=name)
            nc.scalar.activation(got[:], window[:].indirect(offsets), COPY)
            return got

        left0 = vector_gather("left0", a, half(0, 0))
        right0 = scalar_gather("right0", a, half(1, 0))
        right1 = scalar_gather("right1", a, half(1, 1))
        left1 = scalar_gather("left1", a, half(0, 1))
        nc.vector.tensor_tensor(f1[:].indirect(half(0, 0)), left0[:], right0[:], ALU.mult)
        nc.vector.tensor_tensor(f1[:].indirect(half(0, 1)), left1[:], right1[:], ALU.mult)

        f2 = keep.tile([P, T], F32)
        banks_old = []
        for b, (c0, c1) in enumerate(((0, 512), (512, PSUM_SHARE))):
            blocks = (c1 - c0 + P - 1) // P
            turned = psum.tile([P, blocks, P], F32, name=f"turned{b}", tag=f"bank{b}")
            for j in range(blocks):
                nc.tensor.transpose(turned[:, j, :], old_sb[:, c0 + j * P : c0 + (j + 1) * P], ident[:])
            old_t = keep.tile([P, blocks, P], F32, name=f"old_t{b}")
            nc.scalar.copy(old_t[:], turned[:])
            back = psum.tile([P, blocks * P], F32, name=f"back{b}", tag=f"bank{b + 2}")
            for j in range(blocks):
                nc.tensor.transpose(back[:, j * P : (j + 1) * P], old_t[:, j, :], ident[:])
            banks_old.append((c0, c1, back))
        nc.gpsimd.tensor_tensor(f2[:, PSUM_SHARE:], f1[:, PSUM_SHARE:], old_sb[:, PSUM_SHARE:], ALU.add)
        for c0, c1, back in banks_old:
            nc.vector.tensor_tensor(f2[:, c0:c1], f1[:, c0:c1], back[:, : c1 - c0], ALU.add)


        third = [vector_gather(f"third{h}", f2, half(2, h)) for h in range(2)]
        fourth = [scalar_gather(f"fourth{h}", f2, half(3, h)) for h in range(2)]
        for s, (c0, c1) in enumerate(STORES):
            h, r0 = divmod(c0, HALF)
            y = keep.tile([P, c1 - c0], F32, name=f"y{s}")
            part = slice(r0, r0 + c1 - c0)
            nc.vector.tensor_tensor(y[:], third[h][:, part], fourth[h][:, part], ALU.max)
            queue = nc.sync if s % 2 == 0 else nc.scalar
            queue.dma_start(out=out[:, c0:c1], in_=y[:])
